import numpy as np
import ml_dtypes


def mxq(x, axis, fmt="e4m3"):
    dtype, down = {"e4m3": (ml_dtypes.float8_e4m3fn, 7), "e5m2": (ml_dtypes.float8_e5m2, 14)}[fmt]
    v = np.moveaxis(np.asarray(x, np.float32).astype(ml_dtypes.bfloat16).astype(np.float64), axis, -1)
    blocks = v.reshape(v.shape[:-1] + (-1, 32))
    amax = np.abs(blocks).max(-1, keepdims=True)
    byte = np.maximum(np.where(amax > 0, np.frexp(amax)[1] - 1 + 127, 0) - down, 1)
    scale = np.exp2(byte - 127.0)
    codes = (blocks / scale).astype(np.float32).astype(dtype).astype(np.float64)
    return np.moveaxis((codes * scale).reshape(v.shape), -1, axis)


WIDE = False


def mx_kscale(k):
    if not WIDE:
        return np.ones(k)
    levels = np.array([10, -10, 5, -5, 0])
    if k % 512:
        return np.exp2(np.random.permutation(np.resize(levels, k // 32))).repeat(32)
    a = np.empty((k // 512, 16))
    for p in range(k // 512):
        a[p, :8] = np.random.permutation(np.resize(levels, 8))
        for g in range(8):
            far = levels[np.abs(levels - a[p, g]) >= 10]
            a[p, g + 8] = far[np.random.randint(len(far))]
    return np.exp2(a.ravel()).repeat(32)


def f64(x):
    return np.asarray(x).astype(np.float64)


def striped(idx):
    return np.tile(np.asarray(idx).reshape(-1, 16).T, (8, 1)).astype(np.uint16)


def unstriped(offs):
    return offs[:16].T.reshape(-1).astype(np.int64)


def striped8(idx):
    return np.asarray(idx).reshape(8, -1, 16).transpose(0, 2, 1).reshape(128, -1).astype(np.uint16)


def unstriped8(offs):
    return offs.reshape(8, 16, -1).transpose(0, 2, 1).reshape(8, -1).astype(np.int64)


def pick8(x, idx, run):
    r = np.arange(len(x))
    return x[r[:, None], idx[r % (8 * run) // run]]


E2M1 = np.array([0.0, 0.5, 1.0, 1.5, 2.0, 3.0, 4.0, 6.0, -0.0, -0.5, -1.0, -1.5, -2.0, -3.0, -4.0, -6.0])


def pack_weight(w, fmt):
    k, n = w.shape
    w = f64(np.asarray(w, np.float32).astype(ml_dtypes.bfloat16)).reshape(k // 32, 32, n)
    amax = np.abs(w).max(1)
    if fmt == "e4m3":
        byte = np.frexp(amax)[1] - 1 + 127 - 7
    else:
        mant, ex = np.frexp(amax / 6.0)
        byte = np.where(mant > 0.5, ex, ex - 1) + 127
    byte = np.clip(np.where(amax > 0, byte, 1), 1, 254)
    scaled = (w * np.exp2(127.0 - byte)[:, None, :]).reshape(k, n).astype(np.float32)
    by_word = np.ascontiguousarray(scaled.reshape(k // 512, 128, 4, n).transpose(0, 1, 3, 2))
    if fmt == "e4m3":
        words = by_word.astype(ml_dtypes.float8_e4m3fn).view(np.uint8)
    else:
        c = by_word.astype(ml_dtypes.float4_e2m1fn).view(np.uint8) & 0xF
        words = (c[..., 0::2] | (c[..., 1::2] << 4)).reshape(k // 512, 128, 2 * n)
    return np.ascontiguousarray(words), np.ascontiguousarray(byte.astype(np.uint8).reshape(k // 512, 16, n))


def unpack_weight(words, scales, fmt):
    g, _, n = scales.shape
    words = np.ascontiguousarray(words).reshape(g, 128, n, -1)
    if fmt == "e4m3":
        vals = words.view(ml_dtypes.float8_e4m3fn).astype(np.float64)
    else:
        nib = np.empty((g, 128, n, 4), np.uint8)
        nib[..., 0::2] = words & 0xF
        nib[..., 1::2] = words >> 4
        vals = E2M1[nib]
    vals = vals * np.repeat(np.exp2(scales.astype(np.float64) - 127.0), 8, axis=1)[..., None]
    return vals.transpose(0, 1, 3, 2).reshape(g * 512, n)


K, R, F, T, J, U = 512, 128, 512, 2048, 512, 1024


def setup_inputs():
    n = np.random.standard_normal
    idx = np.random.permutation(T)[:J]
    idx2 = np.stack([np.random.permutation(U)[:J] for _ in range(8)])
    idx3 = np.stack([np.random.permutation(U)[:J] for _ in range(8)])
    fk = mx_kscale(K)
    ff = mx_kscale(F)
    tabp = pack_weight(n((K, T)) / fk[:, None], "e4m3")
    dtabp = pack_weight(n((K, T)) / fk[:, None], "e4m3")
    return {
        "tab_words": tabp[0],
        "tab_scales": tabp[1],
        "w1": (n((K, R)) * 1 / np.sqrt(K) * fk[:, None]).astype(np.float32),
        "gain": (np.random.uniform(0.5, 1.5, (R, 1))).astype(np.float32),
        "ground": (n((R, U)) * 0.7).astype(np.float32),
        "wo": (n((F, R)) * 1 / np.sqrt(F) * ff[:, None]).astype(np.float32),
        "dy": (n((F, U)) / ff[:, None]).astype(np.float32),
        "dtab_words": dtabp[0],
        "dtab_scales": dtabp[1],
        "og": (np.random.uniform(0.7, 2.0, (R, 1))).astype(np.float32),
        "base": (0.3 * n((R, J))).astype(np.float32),
        "offs": striped(idx),
        "offs2": striped8(idx2),
        "offs3": striped8(idx3),
    }


def reference(tab_words, tab_scales, w1, gain, ground, wo, dy, dtab_words, dtab_scales, og, base, offs, offs2, offs3):
    idx = unstriped(offs)
    idx2 = unstriped8(offs2)
    idx3 = unstriped8(offs3)
    tabu = unpack_weight(tab_words, tab_scales, "e4m3")
    dtabu = unpack_weight(dtab_words, dtab_scales, "e4m3")
    w1q = mxq(f64(w1), 0, "e4m3")
    tabidxg = tabu[:, idx]
    a = w1q.T @ tabidxg
    dtabidxg = dtabu[:, idx]
    ta = w1q.T @ dtabidxg
    h1 = a * f64(gain)
    pa = np.zeros((R, U))
    pa[np.arange(R)[:, None], idx2[np.arange(R) % 128 // 16]] = h1
    pb = np.zeros((R, U))
    pb[np.arange(R)[:, None], idx3[np.arange(R) % 128 // 16]] = a
    woq = mxq(f64(wo), 0, "e4m3")
    dyq = mxq(f64(dy), 0, "e4m3")
    c0 = woq.T @ dyq
    xh1 = ta * f64(gain)
    xpa = np.zeros((R, U))
    xpa[np.arange(R)[:, None], idx2[np.arange(R) % 128 // 16]] = xh1
    xpb = np.zeros((R, U))
    xpb[np.arange(R)[:, None], idx3[np.arange(R) % 128 // 16]] = ta
    xdpb = xpa * (1.0 - np.square(np.tanh(pa + f64(ground)))) * c0
    xdpa = xpb * c0 * (1.0 - np.square(np.tanh(pa + f64(ground)))) + xpa * (1.0 - np.square(np.tanh(pa + f64(ground)))) * np.tanh(pa + f64(ground)) * 2.0 * (-1.0) * c0 * (pb + f64(ground))
    xdh1 = pick8(xdpa, idx2, 16)
    xda = pick8(xdpb, idx3, 16) + xdh1 * f64(gain)
    y = xda * f64(og) + f64(base)
    return y

@@ -1,0 +1,259 @@
+from contextlib import ExitStack
+
+import concourse.mybir as mybir
+from concourse.masks import make_identity
+
+K, R, F, T, J, U = 512, 128, 512, 2048, 512, 1024
+FLOPS = 2 * K * R * J * 2 + 2 * F * R * U
+
+F32 = mybir.dt.float32
+BF16 = mybir.dt.bfloat16
+I32 = mybir.dt.int32
+U32 = mybir.dt.uint32
+U16 = mybir.dt.uint16
+U8 = mybir.dt.uint8
+FP8X4 = mybir.dt.float8_e4m3fn_x4
+ALU = mybir.AluOpType
+ACT = mybir.ActivationFunctionType
+
+P = 128
+PACK = 4
+BANK = 512
+HALF = J // 2
+PER_BANK = BANK // P
+
+
+def tile_attend_hvtwopages_kernel(
+    tc, tab_words, tab_scales, w1, gain, ground, wo, dy, dtab_words, dtab_scales, og, base, offs, offs2, offs3, out
+):
+    nc = tc.nc
+    with ExitStack() as ctx:
+        sb = ctx.enter_context(tc.tile_pool(name="sb", bufs=1))
+        ps = ctx.enter_context(tc.psum_pool(name="ps", bufs=1))
+
+        def sbuf(name, shape, dtype):
+            return sb.tile(shape, dtype, name=name, align_bytes=64)
+
+        def bank(name, number):
+            return ps.tile([P, BANK], F32, name=name, tag="bank%d" % number)
+
+        def load_words(name, words):
+            t = sbuf(name, [P, T], U32)
+            nc.sync.dma_start(t[:].bitcast(I32), words[0].rearrange("p n t -> p (n t)").bitcast(I32))
+            return t
+
+        def load_scales(t, scales):
+            for q in range(4):
+                nc.sync.dma_start(t[32 * q : 32 * q + 4, :].bitcast(I32), scales[0, 4 * q : 4 * q + 4, :].bitcast(I32))
+
+        def load_plain(name, src, shape, dtype):
+            t = sbuf(name, shape, dtype)
+            nc.sync.dma_start(t[:], src)
+            return t
+
+        def load_rows(name, src):
+            width = src.shape[1]
+            t = sbuf(name, [P, PACK, width], F32)
+            nc.sync.dma_start(t[:], src.rearrange("(p j) w -> p j w", j=PACK))
+            return t
+
+        def interleave(grouped, raw, cols):
+            nc.scalar.activation(
+                grouped[:, cols, :].rearrange("p (c i) j -> p c j i", i=4),
+                raw[:, :, cols].rearrange("p j (c i) -> p c j i", i=4),
+                ACT.Copy,
+            )
+
+        def quantize(name, grouped):
+            width = grouped.shape[1]
+            codes = sbuf(name + "_codes", [P, width], U32)
+            scales = sbuf(name + "_scales", [P, width], U8)
+            nc.vector.quantize_mx(
+                out=codes[:].bitcast(FP8X4), scales=scales[:], in_=grouped[:].rearrange("p w j -> p (w j)")
+            )
+            return codes, scales
+
+        def product(acc, lhs, rhs_codes, rhs_scales):
+            nc.tensor.matmul_mx(
+                out=acc,
+                lhsT=lhs[0][:].bitcast(FP8X4),
+                lhsT_scale=lhs[1][:],
+                rhs=rhs_codes.bitcast(FP8X4),
+                rhs_scale=rhs_scales,
+                start=True,
+                stop=True,
+            )
+
+        def turn(dst, src, half, start, stop):
+            for b in range(PER_BANK):
+                lo = half * BANK + b * P
+                nc.tensor.matmul(
+                    dst[:, b * P : (b + 1) * P],
+                    lhsT=src[:, lo : lo + P],
+                    rhs=ident[:],
+                    start=start and b == 0,
+                    stop=stop and b == PER_BANK - 1,
+                    is_transpose=True,
+                )
+
+        def halfcols(h):
+            return slice(h * BANK, (h + 1) * BANK)
+
+        ts_sb = sbuf("ts_sb", [P, T], U8)
+        ds_sb = sbuf("ds_sb", [P, T], U8)
+        nc.gpsimd.memset(ts_sb[:].bitcast(I32), 0)
+        nc.vector.memset(ds_sb[:].bitcast(I32), 0)
+        pb = sbuf("pb", [P, U], F32)
+        pa = sbuf("pa", [P, U], F32)
+        xpb = sbuf("xpb", [P, U], F32)
+        xpa = sbuf("xpa", [P, U], F32)
+        for page in (pb, pa, xpb, xpa):
+            nc.vector.memset(page[:], 0.0)
+        ident = sbuf("ident", [P, P], F32)
+        make_identity(nc, ident[:])
+
+        list1 = load_plain("list1", offs, [P, J // 16], U16)
+        w1_raw = load_rows("w1_raw", w1)
+        list3 = load_plain("list3", offs3, [P, J // 16], U16)
+        load_scales(ts_sb, tab_scales)
+        tw_sb = load_words("tw_sb", tab_words)
+        load_scales(ds_sb, dtab_scales)
+        list2 = load_plain("list2", offs2, [P, J // 16], U16)
+        gain_sb = sbuf("gain_sb", [P, 1], F32)
+        nc.sync.dma_start(gain_sb[:], gain)
+        og_sb = sbuf("og_sb", [P, 1], F32)
+        nc.sync.dma_start(og_sb[:], og)
+        dw_sb = load_words("dw_sb", dtab_words)
+        ground_sb = load_plain("ground_sb", ground, [P, U], F32)
+        wo_raw = load_rows("wo_raw", wo)
+        dy_raw = [load_rows("dy_raw%d" % h, dy[:, halfcols(h)]) for h in range(2)]
+        base_sb = load_plain("base_sb", base, [P, J], F32)
+
+        w1_grouped = sbuf("w1_grouped", [P, R, PACK], BF16)
+        interleave(w1_grouped, w1_raw, slice(0, R))
+        ts_g = sbuf("ts_g", [P, J], U8)
+        nc.vector.tensor_copy(ts_g[:], ts_sb[:].indirect(list1[:]))
+        w1_q = quantize("w1", w1_grouped)
+        tw_g = sbuf("tw_g", [P, J], U32)
+        a_sb = sbuf("a_sb", [P, J], F32)
+        h1_sb = sbuf("h1_sb", [P, J], F32)
+        a_ps = []
+        for h in range(2):
+            slots = slice(h * HALF, (h + 1) * HALF)
+            entries = slice(h * HALF // 16, (h + 1) * HALF // 16)
+            nc.vector.tensor_copy(tw_g[:, slots], tw_sb[:].indirect(list1[:, entries]))
+            a_ps.append(bank("a_ps%d" % h, h))
+            product(a_ps[h][:, :HALF], w1_q, tw_g[:, slots], ts_g[:, slots])
+            nc.scalar.copy(a_sb[:, slots], a_ps[h][:, :HALF])
+        for h in range(2):
+            slots = slice(h * HALF, (h + 1) * HALF)
+            nc.scalar.activation(h1_sb[:, slots], a_ps[h][:, :HALF], ACT.Copy, scale=gain_sb[:])
+        ds_g = sbuf("ds_g", [P, J], U8)
+        nc.vector.tensor_copy(ds_g[:], ds_sb[:].indirect(list1[:]))
+        for h in range(2):
+            slots = slice(h * HALF, (h + 1) * HALF)
+            entries = slice(h * HALF // 16, (h + 1) * HALF // 16)
+            nc.vector.tensor_copy(pb[:].indirect(list3[:, entries]), a_sb[:, slots])
+
+        dw_g = sbuf("dw_g", [P, J], U32)
+        nc.vector.tensor_copy(dw_g[:], dw_sb[:].indirect(list1[:]))
+        ta_ps = bank("ta_ps", 0)
+        product(ta_ps[:], w1_q, dw_g[:], ds_g[:])
+        ta_sb = sbuf("ta_sb", [P, J], F32)
+        xh1_sb = sbuf("xh1_sb", [P, J], F32)
+        nc.scalar.copy(ta_sb[:], ta_ps[:])
+        nc.scalar.activation(xh1_sb[:], ta_ps[:], ACT.Copy, scale=gain_sb[:])
+
+        nc.vector.tensor_copy(pa[:].indirect(list2[:]), h1_sb[:])
+
+        q_ps = [bank("q_ps%d" % h, 2 + h) for h in range(2)]
+        for h in range(2):
+            turn(q_ps[h], ground_sb, h, True, False)
+            turn(q_ps[h], pb, h, False, True)
+        z_ps = [bank("z_ps%d" % h, 4 + h) for h in range(2)]
+        tanh_t = sbuf("tanh_t", [P, U], F32)
+        for h in range(2):
+            turn(z_ps[h], ground_sb, h, True, False)
+            turn(z_ps[h], pa, h, False, True)
+
+        wo_grouped = sbuf("wo_grouped", [P, R, PACK], BF16)
+        interleave(wo_grouped, wo_raw, slice(0, R))
+        wo_q = quantize("wo", wo_grouped)
+        c0_ps = []
+        for h in range(2):
+            grouped = sbuf("dy_grouped%d" % h, [P, BANK, PACK], BF16)
+            for c in range(2):
+                interleave(grouped, dy_raw[h], slice(c * 256, (c + 1) * 256))
+            dy_q = quantize("dy%d" % h, grouped)
+            c0_ps.append(bank("c0_ps%d" % h, 6 + h))
+            product(c0_ps[h][:], wo_q, dy_q[0][:], dy_q[1][:])
+
+        nc.vector.tensor_copy(xpb[:].indirect(list3[:]), ta_sb[:])
+
+        for h in range(2):
+            nc.scalar.activation(tanh_t[:, halfcols(h)], z_ps[h][:], ACT.Tanh)
+        tanh_sq = sbuf("tanh_sq", [P, U], F32)
+        for h in range(2):
+            back = bank("back%d" % h, h)
+            turn(back, tanh_t, h, True, True)
+            nc.scalar.activation(tanh_sq[:, halfcols(h)], back[:], ACT.Square)
+
+        xpb_t = sbuf("xpb_t", [P, U], F32)
+        for h in range(2):
+            turned = bank("xpb_ps%d" % h, 4 + h)
+            turn(turned, xpb, h, True, True)
+            nc.scalar.copy(xpb_t[:, halfcols(h)], turned[:])
+
+        m_t = sbuf("m_t", [P, U], F32)
+        for h in range(2):
+            nc.vector.scalar_tensor_tensor(
+                m_t[:, halfcols(h)], q_ps[h][:], -2.0, tanh_t[:, halfcols(h)], ALU.mult, ALU.mult
+            )
+
+        nc.vector.tensor_copy(xpa[:].indirect(list2[:]), xh1_sb[:])
+
+        ncs = sbuf("ncs", [P, U], F32)
+        for h in range(2):
+            nc.vector.scalar_tensor_tensor(
+                ncs[:, halfcols(h)], tanh_sq[:, halfcols(h)], 1.0, c0_ps[h][:], ALU.subtract, ALU.mult
+            )
+
+        gain_wide = sbuf("gain_wide", [P, J], F32)
+        nc.scalar.copy(gain_wide[:], gain_sb[:].to_broadcast([P, J]))
+
+        sum_ps = [bank("sum_ps%d" % h, h) for h in range(2)]
+        for h in range(2):
+            turn(sum_ps[h], xpb_t, h, True, False)
+        xpa_ps = [bank("xpa_ps%d" % h, 2 + h) for h in range(2)]
+        for h in range(2):
+            turn(xpa_ps[h], xpa, h, True, True)
+
+        w_t = sbuf("w_t", [P, U], F32)
+        xdpb = sbuf("xdpb", [P, U], F32)
+        xdpa = sbuf("xdpa", [P, U], F32)
+        for h in range(2):
+            nc.vector.tensor_tensor(w_t[:, halfcols(h)], xpa_ps[h][:], m_t[:, halfcols(h)], ALU.mult)
+            turn(sum_ps[h], w_t, h, False, True)
+        nc.vector.scalar_tensor_tensor(xdpb[:], xpa[:], -1.0, ncs[:], ALU.mult, ALU.mult)
+        for h in range(2):
+            nc.vector.scalar_tensor_tensor(
+                xdpa[:, halfcols(h)], sum_ps[h][:], -1.0, ncs[:, halfcols(h)], ALU.mult, ALU.mult
+            )
+
+        scaled = sbuf("scaled", [P, J], F32)
+        xda = sbuf("xda", [P, J], F32)
+        result = sbuf("result", [P, J], F32)
+        for h in range(2):
+            slots = slice(h * HALF, (h + 1) * HALF)
+            entries = slice(h * HALF // 16, (h + 1) * HALF // 16)
+            nc.vector.tensor_tensor(scaled[:, slots], xdpa[:].indirect(list2[:, entries]), gain_wide[:, slots], ALU.mult)
+        for h in range(2):
+            slots = slice(h * HALF, (h + 1) * HALF)
+            entries = slice(h * HALF // 16, (h + 1) * HALF // 16)
+            nc.vector.tensor_tensor(xda[:, slots], xdpb[:].indirect(list3[:, entries]), scaled[:, slots], ALU.add)
+        for h in range(2):
+            slots = slice(h * HALF, (h + 1) * HALF)
+            nc.vector.scalar_tensor_tensor(
+                result[:, slots], xda[:, slots], og_sb[:], base_sb[:, slots], ALU.mult, ALU.add
+            )
+            nc.sync.dma_start(out[:, slots], result[:, slots])

@@ -31,8 +31,8 @@ def tile_attend_hvtwopages_kernel(
         sb = ctx.enter_context(tc.tile_pool(name="sb", bufs=1))
         ps = ctx.enter_context(tc.psum_pool(name="ps", bufs=1))
 
-        def sbuf(name, shape, dtype):
-            return sb.tile(shape, dtype, name=name, align_bytes=64)
+        def sbuf(name, shape, dtype, tag=""):
+            return sb.tile(shape, dtype, name=name, align_bytes=64, tag=tag or name)
 
         def bank(name, number):
             return ps.tile([P, BANK], F32, name=name, tag="bank%d" % number)
@@ -108,7 +108,7 @@ def tile_attend_hvtwopages_kernel(
         xpb = sbuf("xpb", [P, U], F32)
         xpa = sbuf("xpa", [P, U], F32)
         for page in (pb, pa, xpb, xpa):
-            nc.vector.memset(page[:], 0.0)
+            nc.vector.memset(page[:].bitcast(I32), 0)
         ident = sbuf("ident", [P, P], F32)
         make_identity(nc, ident[:])
 
@@ -118,15 +118,13 @@ def tile_attend_hvtwopages_kernel(
         load_scales(ts_sb, tab_scales)
         tw_sb = load_words("tw_sb", tab_words)
         load_scales(ds_sb, dtab_scales)
-        list2 = load_plain("list2", offs2, [P, J // 16], U16)
-        gain_sb = sbuf("gain_sb", [P, 1], F32)
-        nc.sync.dma_start(gain_sb[:], gain)
-        og_sb = sbuf("og_sb", [P, 1], F32)
-        nc.sync.dma_start(og_sb[:], og)
         dw_sb = load_words("dw_sb", dtab_words)
-        ground_sb = load_plain("ground_sb", ground, [P, U], F32)
+        list2 = load_plain("list2", offs2, [P, J // 16], U16)
+        gain_sb = load_plain("gain_sb", gain, [P, 1], F32)
         wo_raw = load_rows("wo_raw", wo)
         dy_raw = [load_rows("dy_raw%d" % h, dy[:, halfcols(h)]) for h in range(2)]
+        ground_sb = load_plain("ground_sb", ground, [P, U], F32)
+        og_sb = load_plain("og_sb", og, [P, 1], F32)
         base_sb = load_plain("base_sb", base, [P, J], F32)
 
         w1_grouped = sbuf("w1_grouped", [P, R, PACK], BF16)
@@ -157,39 +155,46 @@ def tile_attend_hvtwopages_kernel(
 
         dw_g = sbuf("dw_g", [P, J], U32)
         nc.vector.tensor_copy(dw_g[:], dw_sb[:].indirect(list1[:]))
-        ta_ps = bank("ta_ps", 0)
-        product(ta_ps[:], w1_q, dw_g[:], ds_g[:])
-        ta_sb = sbuf("ta_sb", [P, J], F32)
-        xh1_sb = sbuf("xh1_sb", [P, J], F32)
-        nc.scalar.copy(ta_sb[:], ta_ps[:])
-        nc.scalar.activation(xh1_sb[:], ta_ps[:], ACT.Copy, scale=gain_sb[:])
-
+        ta_ps = [bank("ta_ps%d" % h, 4 + h) for h in range(2)]
+        for h in range(2):
+            slots = slice(h * HALF, (h + 1) * HALF)
+            product(ta_ps[h][:, :HALF], w1_q, dw_g[:, slots], ds_g[:, slots])
         nc.vector.tensor_copy(pa[:].indirect(list2[:]), h1_sb[:])
+
+        wo_grouped = sbuf("wo_grouped", [P, R, PACK], BF16)
+        interleave(wo_grouped, wo_raw, slice(0, R))
+        wo_q = quantize("wo", wo_grouped)
+
+        def group_dy(h):
+            grouped = sbuf("dy_grouped%d" % h, [P, BANK, PACK], BF16)
+            for c in range(2):
+                interleave(grouped, dy_raw[h], slice(c * 256, (c + 1) * 256))
+            return grouped
+
+        dy_grouped = [group_dy(0)]
+        xh1_sb = sbuf("xh1_sb", [P, J], F32, tag="dy_raw0")
+        for h in range(2):
+            slots = slice(h * HALF, (h + 1) * HALF)
+            nc.scalar.activation(xh1_sb[:, slots], ta_ps[h][:, :HALF], ACT.Copy, scale=gain_sb[:])
+        nc.vector.tensor_copy(xpa[:].indirect(list2[:]), xh1_sb[:])
+        dy_grouped.append(group_dy(1))
+        ta_sb = sbuf("ta_sb", [P, J], F32, tag="dy_raw1")
+        for h in range(2):
+            slots = slice(h * HALF, (h + 1) * HALF)
+            nc.scalar.copy(ta_sb[:, slots], ta_ps[h][:, :HALF])
+        nc.vector.tensor_copy(xpb[:].indirect(list3[:]), ta_sb[:])
+        dy_q = [quantize("dy%d" % h, dy_grouped[h]) for h in range(2)]
 
         q_ps = [bank("q_ps%d" % h, 2 + h) for h in range(2)]
         for h in range(2):
             turn(q_ps[h], ground_sb, h, True, False)
             turn(q_ps[h], pb, h, False, True)
         z_ps = [bank("z_ps%d" % h, 4 + h) for h in range(2)]
-        tanh_t = sbuf("tanh_t", [P, U], F32)
         for h in range(2):
             turn(z_ps[h], ground_sb, h, True, False)
             turn(z_ps[h], pa, h, False, True)
 
-        wo_grouped = sbuf("wo_grouped", [P, R, PACK], BF16)
-        interleave(wo_grouped, wo_raw, slice(0, R))
-        wo_q = quantize("wo", wo_grouped)
-        c0_ps = []
-        for h in range(2):
-            grouped = sbuf("dy_grouped%d" % h, [P, BANK, PACK], BF16)
-            for c in range(2):
-                interleave(grouped, dy_raw[h], slice(c * 256, (c + 1) * 256))
-            dy_q = quantize("dy%d" % h, grouped)
-            c0_ps.append(bank("c0_ps%d" % h, 6 + h))
-            product(c0_ps[h][:], wo_q, dy_q[0][:], dy_q[1][:])
-
-        nc.vector.tensor_copy(xpb[:].indirect(list3[:]), ta_sb[:])
-
+        tanh_t = sbuf("tanh_t", [P, U], F32)
         for h in range(2):
             nc.scalar.activation(tanh_t[:, halfcols(h)], z_ps[h][:], ACT.Tanh)
         tanh_sq = sbuf("tanh_sq", [P, U], F32)
@@ -198,35 +203,31 @@ def tile_attend_hvtwopages_kernel(
             turn(back, tanh_t, h, True, True)
             nc.scalar.activation(tanh_sq[:, halfcols(h)], back[:], ACT.Square)
 
+        xpa_ps = [bank("xpa_ps%d" % h, 4 + h) for h in range(2)]
+        for h in range(2):
+            turn(xpa_ps[h], xpa, h, True, True)
+
         xpb_t = sbuf("xpb_t", [P, U], F32)
         for h in range(2):
-            turned = bank("xpb_ps%d" % h, 4 + h)
+            turned = bank("xpb_ps%d" % h, h)
             turn(turned, xpb, h, True, True)
             nc.scalar.copy(xpb_t[:, halfcols(h)], turned[:])
 
+        c0_ps = []
         m_t = sbuf("m_t", [P, U], F32)
         for h in range(2):
             nc.vector.scalar_tensor_tensor(
                 m_t[:, halfcols(h)], q_ps[h][:], -2.0, tanh_t[:, halfcols(h)], ALU.mult, ALU.mult
             )
-
-        nc.vector.tensor_copy(xpa[:].indirect(list2[:]), xh1_sb[:])
-
-        ncs = sbuf("ncs", [P, U], F32)
-        for h in range(2):
-            nc.vector.scalar_tensor_tensor(
-                ncs[:, halfcols(h)], tanh_sq[:, halfcols(h)], 1.0, c0_ps[h][:], ALU.subtract, ALU.mult
-            )
+            c0_ps.append(bank("c0_ps%d" % h, 2 + h))
+            product(c0_ps[h][:], wo_q, dy_q[h][0][:], dy_q[h][1][:])
 
         gain_wide = sbuf("gain_wide", [P, J], F32)
         nc.scalar.copy(gain_wide[:], gain_sb[:].to_broadcast([P, J]))
 
-        sum_ps = [bank("sum_ps%d" % h, h) for h in range(2)]
+        sum_ps = [bank("sum_ps%d" % h, 6 + h) for h in range(2)]
         for h in range(2):
             turn(sum_ps[h], xpb_t, h, True, False)
-        xpa_ps = [bank("xpa_ps%d" % h, 2 + h) for h in range(2)]
-        for h in range(2):
-            turn(xpa_ps[h], xpa, h, True, True)
 
         w_t = sbuf("w_t", [P, U], F32)
         xdpb = sbuf("xdpb", [P, U], F32)
@@ -234,6 +235,12 @@ def tile_attend_hvtwopages_kernel(
         for h in range(2):
             nc.vector.tensor_tensor(w_t[:, halfcols(h)], xpa_ps[h][:], m_t[:, halfcols(h)], ALU.mult)
             turn(sum_ps[h], w_t, h, False, True)
+        ncs = sbuf("ncs", [P, U], F32)
+        for h in range(2):
+            nc.vector.scalar_tensor_tensor(
+                ncs[:, halfcols(h)], tanh_sq[:, halfcols(h)], 1.0, c0_ps[h][:], ALU.subtract, ALU.mult
+            )
+
         nc.vector.scalar_tensor_tensor(xdpb[:], xpa[:], -1.0, ncs[:], ALU.mult, ALU.mult)
         for h in range(2):
             nc.vector.scalar_tensor_tensor(

@@ -57,10 +57,10 @@ def tile_attend_hvtwopages_kernel(
             nc.sync.dma_start(t[:], src.rearrange("(p j) w -> p j w", j=PACK))
             return t
 
-        def interleave(grouped, raw, cols):
+        def interleave(grouped, raw):
             nc.scalar.activation(
-                grouped[:, cols, :].rearrange("p (c i) j -> p c j i", i=4),
-                raw[:, :, cols].rearrange("p j (c i) -> p c j i", i=4),
+                grouped.rearrange("p (c i) j -> p c j i", i=4),
+                raw.rearrange("p j (c i) -> p c j i", i=4),
                 ACT.Copy,
             )
 
@@ -122,13 +122,14 @@ def tile_attend_hvtwopages_kernel(
         list2 = load_plain("list2", offs2, [P, J // 16], U16)
         gain_sb = load_plain("gain_sb", gain, [P, 1], F32)
         wo_raw = load_rows("wo_raw", wo)
-        dy_raw = [load_rows("dy_raw%d" % h, dy[:, halfcols(h)]) for h in range(2)]
+        dy_raw = [load_rows("dy_raw%d" % c, dy[:, c * 256 : (c + 1) * 256]) for c in range(2)]
         ground_sb = load_plain("ground_sb", ground, [P, U], F32)
+        dy_raw.extend([load_rows("dy_raw%d" % c, dy[:, c * 256 : (c + 1) * 256]) for c in range(2, 4)])
         og_sb = load_plain("og_sb", og, [P, 1], F32)
         base_sb = load_plain("base_sb", base, [P, J], F32)
 
         w1_grouped = sbuf("w1_grouped", [P, R, PACK], BF16)
-        interleave(w1_grouped, w1_raw, slice(0, R))
+        interleave(w1_grouped[:], w1_raw[:])
         ts_g = sbuf("ts_g", [P, J], U8)
         nc.vector.tensor_copy(ts_g[:], ts_sb[:].indirect(list1[:]))
         w1_q = quantize("w1", w1_grouped)
@@ -155,72 +156,65 @@ def tile_attend_hvtwopages_kernel(
 
         dw_g = sbuf("dw_g", [P, J], U32)
         nc.vector.tensor_copy(dw_g[:], dw_sb[:].indirect(list1[:]))
-        ta_ps = [bank("ta_ps%d" % h, 4 + h) for h in range(2)]
-        for h in range(2):
-            slots = slice(h * HALF, (h + 1) * HALF)
-            product(ta_ps[h][:, :HALF], w1_q, dw_g[:, slots], ds_g[:, slots])
+        ta_ps = bank("ta_ps", 6)
+        product(ta_ps[:], w1_q, dw_g[:], ds_g[:])
         nc.vector.tensor_copy(pa[:].indirect(list2[:]), h1_sb[:])
 
         wo_grouped = sbuf("wo_grouped", [P, R, PACK], BF16)
-        interleave(wo_grouped, wo_raw, slice(0, R))
+        interleave(wo_grouped[:], wo_raw[:])
         wo_q = quantize("wo", wo_grouped)
 
-        def group_dy(h):
-            grouped = sbuf("dy_grouped%d" % h, [P, BANK, PACK], BF16)
+        dy_grouped = [sbuf("dy_grouped%d" % h, [P, BANK, PACK], BF16) for h in range(2)]
+        dy_q = []
+        for h in range(2):
             for c in range(2):
-                interleave(grouped, dy_raw[h], slice(c * 256, (c + 1) * 256))
-            return grouped
-
-        dy_grouped = [group_dy(0)]
-        xh1_sb = sbuf("xh1_sb", [P, J], F32, tag="dy_raw0")
-        for h in range(2):
-            slots = slice(h * HALF, (h + 1) * HALF)
-            nc.scalar.activation(xh1_sb[:, slots], ta_ps[h][:, :HALF], ACT.Copy, scale=gain_sb[:])
-        nc.vector.tensor_copy(xpa[:].indirect(list2[:]), xh1_sb[:])
-        dy_grouped.append(group_dy(1))
-        ta_sb = sbuf("ta_sb", [P, J], F32, tag="dy_raw1")
-        for h in range(2):
-            slots = slice(h * HALF, (h + 1) * HALF)
-            nc.scalar.copy(ta_sb[:, slots], ta_ps[h][:, :HALF])
-        nc.vector.tensor_copy(xpb[:].indirect(list3[:]), ta_sb[:])
-        dy_q = [quantize("dy%d" % h, dy_grouped[h]) for h in range(2)]
+                interleave(dy_grouped[h][:, c * 256 : (c + 1) * 256, :], dy_raw[2 * h + c][:])
+            dy_q.append(quantize("dy%d" % h, dy_grouped[h]))
+        late = sbuf("late", [P, 2 * J + 2 * U], F32, tag="dy_raw3")
+        ta_sb = late[:, :J]
+        xh1_sb = late[:, J : 2 * J]
+        q_t = late[:, 2 * J : 2 * J + U]
+        tanh_t = late[:, 2 * J + U :]
+        nc.scalar.copy(ta_sb, ta_ps[:])
+        nc.vector.tensor_copy(xpb[:].indirect(list3[:]), ta_sb)
+        nc.scalar.activation(xh1_sb, ta_ps[:], ACT.Copy, scale=gain_sb[:])
+        nc.vector.tensor_copy(xpa[:].indirect(list2[:]), xh1_sb)
 
         q_ps = [bank("q_ps%d" % h, 2 + h) for h in range(2)]
-        for h in range(2):
-            turn(q_ps[h], ground_sb, h, True, False)
-            turn(q_ps[h], pb, h, False, True)
         z_ps = [bank("z_ps%d" % h, 4 + h) for h in range(2)]
         for h in range(2):
             turn(z_ps[h], ground_sb, h, True, False)
-            turn(z_ps[h], pa, h, False, True)
-
-        tanh_t = sbuf("tanh_t", [P, U], F32)
+        turn(q_ps[0], ground_sb, 0, True, False)
+        turn(q_ps[0], pb, 0, False, True)
+        nc.scalar.activation(q_t[:, halfcols(0)], q_ps[0][:], ACT.Copy, scale=-2.0)
         for h in range(2):
+            turn(z_ps[h], pa, h, False, True)
             nc.scalar.activation(tanh_t[:, halfcols(h)], z_ps[h][:], ACT.Tanh)
+        turn(q_ps[1], ground_sb, 1, True, False)
+        turn(q_ps[1], pb, 1, False, True)
+        nc.scalar.activation(q_t[:, halfcols(1)], q_ps[1][:], ACT.Copy, scale=-2.0)
+        slope = sbuf("slope", [P, U], F32)
         tanh_sq = sbuf("tanh_sq", [P, U], F32)
         for h in range(2):
             back = bank("back%d" % h, h)
             turn(back, tanh_t, h, True, True)
             nc.scalar.activation(tanh_sq[:, halfcols(h)], back[:], ACT.Square)
-
-        xpa_ps = [bank("xpa_ps%d" % h, 4 + h) for h in range(2)]
         for h in range(2):
-            turn(xpa_ps[h], xpa, h, True, True)
+            nc.scalar.activation(slope[:, halfcols(h)], tanh_sq[:, halfcols(h)], ACT.Copy, scale=-1.0, bias=1.0)
+
+        m_t = sbuf("m_t", [P, U], F32, tag="dy_grouped0")
+        for h in range(2):
+            nc.gpsimd.tensor_tensor(m_t[:, halfcols(h)], q_t[:, halfcols(h)], tanh_t[:, halfcols(h)], ALU.mult)
+
+        c0_ps = [bank("c0_ps%d" % h, 2 + h) for h in range(2)]
+        for h in range(2):
+            product(c0_ps[h][:], wo_q, dy_q[h][0][:], dy_q[h][1][:])
 
         xpb_t = sbuf("xpb_t", [P, U], F32)
         for h in range(2):
-            turned = bank("xpb_ps%d" % h, h)
+            turned = bank("xpb_ps%d" % h, 4 + h)
             turn(turned, xpb, h, True, True)
             nc.scalar.copy(xpb_t[:, halfcols(h)], turned[:])
-
-        c0_ps = []
-        m_t = sbuf("m_t", [P, U], F32)
-        for h in range(2):
-            nc.vector.scalar_tensor_tensor(
-                m_t[:, halfcols(h)], q_ps[h][:], -2.0, tanh_t[:, halfcols(h)], ALU.mult, ALU.mult
-            )
-            c0_ps.append(bank("c0_ps%d" % h, 2 + h))
-            product(c0_ps[h][:], wo_q, dy_q[h][0][:], dy_q[h][1][:])
 
         gain_wide = sbuf("gain_wide", [P, J], F32)
         nc.scalar.copy(gain_wide[:], gain_sb[:].to_broadcast([P, J]))
@@ -228,24 +222,22 @@ def tile_attend_hvtwopages_kernel(
         sum_ps = [bank("sum_ps%d" % h, 6 + h) for h in range(2)]
         for h in range(2):
             turn(sum_ps[h], xpb_t, h, True, False)
+        xpa_ps = [bank("xpa_ps%d" % h, 4 + h) for h in range(2)]
+        for h in range(2):
+            turn(xpa_ps[h], xpa, h, True, True)
 
+        cs = sbuf("cs", [P, U], F32)
         w_t = sbuf("w_t", [P, U], F32)
         xdpb = sbuf("xdpb", [P, U], F32)
         xdpa = sbuf("xdpa", [P, U], F32)
         for h in range(2):
+            nc.vector.tensor_tensor(cs[:, halfcols(h)], c0_ps[h][:], slope[:, halfcols(h)], ALU.mult)
+            nc.gpsimd.tensor_tensor(xdpb[:, halfcols(h)], xpa[:, halfcols(h)], cs[:, halfcols(h)], ALU.mult)
+        for h in range(2):
             nc.vector.tensor_tensor(w_t[:, halfcols(h)], xpa_ps[h][:], m_t[:, halfcols(h)], ALU.mult)
             turn(sum_ps[h], w_t, h, False, True)
-        ncs = sbuf("ncs", [P, U], F32)
         for h in range(2):
-            nc.vector.scalar_tensor_tensor(
-                ncs[:, halfcols(h)], tanh_sq[:, halfcols(h)], 1.0, c0_ps[h][:], ALU.subtract, ALU.mult
-            )
-
-        nc.vector.scalar_tensor_tensor(xdpb[:], xpa[:], -1.0, ncs[:], ALU.mult, ALU.mult)
-        for h in range(2):
-            nc.vector.scalar_tensor_tensor(
-                xdpa[:, halfcols(h)], sum_ps[h][:], -1.0, ncs[:, halfcols(h)], ALU.mult, ALU.mult
-            )
+            nc.vector.tensor_tensor(xdpa[:, halfcols(h)], sum_ps[h][:], cs[:, halfcols(h)], ALU.mult)
 
         scaled = sbuf("scaled", [P, J], F32)
         xda = sbuf("xda", [P, J], F32)

@@ -122,9 +122,9 @@ def tile_attend_hvtwopages_kernel(
         list2 = load_plain("list2", offs2, [P, J // 16], U16)
         gain_sb = load_plain("gain_sb", gain, [P, 1], F32)
         wo_raw = load_rows("wo_raw", wo)
-        dy_raw = [load_rows("dy_raw%d" % c, dy[:, c * 256 : (c + 1) * 256]) for c in range(2)]
+        dy_raw = [load_rows("dy_raw0", dy[:, halfcols(0)])]
         ground_sb = load_plain("ground_sb", ground, [P, U], F32)
-        dy_raw.extend([load_rows("dy_raw%d" % c, dy[:, c * 256 : (c + 1) * 256]) for c in range(2, 4)])
+        dy_raw.append(load_rows("dy_raw1", dy[:, halfcols(1)]))
         og_sb = load_plain("og_sb", og, [P, 1], F32)
         base_sb = load_plain("base_sb", base, [P, J], F32)
 
@@ -168,15 +168,16 @@ def tile_attend_hvtwopages_kernel(
         dy_q = []
         for h in range(2):
             for c in range(2):
-                interleave(dy_grouped[h][:, c * 256 : (c + 1) * 256, :], dy_raw[2 * h + c][:])
+                cols = slice(c * 256, (c + 1) * 256)
+                interleave(dy_grouped[h][:, cols, :], dy_raw[h][:, :, cols])
             dy_q.append(quantize("dy%d" % h, dy_grouped[h]))
-        late = sbuf("late", [P, 2 * J + 2 * U], F32, tag="dy_raw3")
-        ta_sb = late[:, :J]
-        xh1_sb = late[:, J : 2 * J]
-        q_t = late[:, 2 * J : 2 * J + U]
-        tanh_t = late[:, 2 * J + U :]
-        nc.scalar.copy(ta_sb, ta_ps[:])
-        nc.vector.tensor_copy(xpb[:].indirect(list3[:]), ta_sb)
+            if h == 0:
+                ta_sb = sbuf("ta_sb", [P, J], F32, tag="dy_raw0")
+                nc.scalar.copy(ta_sb[:], ta_ps[:])
+                nc.vector.tensor_copy(xpb[:].indirect(list3[:]), ta_sb[:])
+        late = sbuf("late", [P, J + U], F32, tag="dy_raw1")
+        xh1_sb = late[:, :J]
+        tanh_t = late[:, J:]
         nc.scalar.activation(xh1_sb, ta_ps[:], ACT.Copy, scale=gain_sb[:])
         nc.vector.tensor_copy(xpa[:].indirect(list2[:]), xh1_sb)
 
@@ -184,15 +185,12 @@ def tile_attend_hvtwopages_kernel(
         z_ps = [bank("z_ps%d" % h, 4 + h) for h in range(2)]
         for h in range(2):
             turn(z_ps[h], ground_sb, h, True, False)
-        turn(q_ps[0], ground_sb, 0, True, False)
-        turn(q_ps[0], pb, 0, False, True)
-        nc.scalar.activation(q_t[:, halfcols(0)], q_ps[0][:], ACT.Copy, scale=-2.0)
         for h in range(2):
             turn(z_ps[h], pa, h, False, True)
             nc.scalar.activation(tanh_t[:, halfcols(h)], z_ps[h][:], ACT.Tanh)
-        turn(q_ps[1], ground_sb, 1, True, False)
-        turn(q_ps[1], pb, 1, False, True)
-        nc.scalar.activation(q_t[:, halfcols(1)], q_ps[1][:], ACT.Copy, scale=-2.0)
+        for h in range(2):
+            turn(q_ps[h], ground_sb, h, True, False)
+            turn(q_ps[h], pb, h, False, True)
         slope = sbuf("slope", [P, U], F32)
         tanh_sq = sbuf("tanh_sq", [P, U], F32)
         for h in range(2):
@@ -202,11 +200,7 @@ def tile_attend_hvtwopages_kernel(
         for h in range(2):
             nc.scalar.activation(slope[:, halfcols(h)], tanh_sq[:, halfcols(h)], ACT.Copy, scale=-1.0, bias=1.0)
 
-        m_t = sbuf("m_t", [P, U], F32, tag="dy_grouped0")
-        for h in range(2):
-            nc.gpsimd.tensor_tensor(m_t[:, halfcols(h)], q_t[:, halfcols(h)], tanh_t[:, halfcols(h)], ALU.mult)
-
-        c0_ps = [bank("c0_ps%d" % h, 2 + h) for h in range(2)]
+        c0_ps = [bank("c0_ps%d" % h, h) for h in range(2)]
         for h in range(2):
             product(c0_ps[h][:], wo_q, dy_q[h][0][:], dy_q[h][1][:])
 
@@ -216,15 +210,17 @@ def tile_attend_hvtwopages_kernel(
             turn(turned, xpb, h, True, True)
             nc.scalar.copy(xpb_t[:, halfcols(h)], turned[:])
 
-        gain_wide = sbuf("gain_wide", [P, J], F32)
-        nc.scalar.copy(gain_wide[:], gain_sb[:].to_broadcast([P, J]))
+        og_wide = sbuf("og_wide", [P, J], F32)
+        nc.scalar.copy(og_wide[:], og_sb[:].to_broadcast([P, J]))
+        both_wide = sbuf("both_wide", [P, J], F32)
+        nc.scalar.activation(both_wide[:], og_wide[:], ACT.Copy, scale=gain_sb[:])
 
-        sum_ps = [bank("sum_ps%d" % h, 6 + h) for h in range(2)]
-        for h in range(2):
-            turn(sum_ps[h], xpb_t, h, True, False)
         xpa_ps = [bank("xpa_ps%d" % h, 4 + h) for h in range(2)]
         for h in range(2):
             turn(xpa_ps[h], xpa, h, True, True)
+        sum_ps = [bank("sum_ps%d" % h, 6 + h) for h in range(2)]
+        for h in range(2):
+            turn(sum_ps[h], xpb_t, h, True, False)
 
         cs = sbuf("cs", [P, U], F32)
         w_t = sbuf("w_t", [P, U], F32)
@@ -233,26 +229,30 @@ def tile_attend_hvtwopages_kernel(
         for h in range(2):
             nc.vector.tensor_tensor(cs[:, halfcols(h)], c0_ps[h][:], slope[:, halfcols(h)], ALU.mult)
             nc.gpsimd.tensor_tensor(xdpb[:, halfcols(h)], xpa[:, halfcols(h)], cs[:, halfcols(h)], ALU.mult)
+        m_t = slope
+        for h in range(2):
+            nc.vector.scalar_tensor_tensor(
+                m_t[:, halfcols(h)], q_ps[h][:], -2.0, tanh_t[:, halfcols(h)], ALU.mult, ALU.mult
+            )
         for h in range(2):
             nc.vector.tensor_tensor(w_t[:, halfcols(h)], xpa_ps[h][:], m_t[:, halfcols(h)], ALU.mult)
             turn(sum_ps[h], w_t, h, False, True)
+        from_b = slope[:, :J]
+        partial = sbuf("partial", [P, J], F32)
+        nc.vector.tensor_tensor(from_b, xdpb[:].indirect(list3[:]), og_wide[:], ALU.mult)
+        for h in range(2):
+            slots = slice(h * HALF, (h + 1) * HALF)
+            nc.gpsimd.tensor_tensor(partial[:, slots], from_b[:, slots], base_sb[:, slots], ALU.add)
         for h in range(2):
             nc.vector.tensor_tensor(xdpa[:, halfcols(h)], sum_ps[h][:], cs[:, halfcols(h)], ALU.mult)
 
-        scaled = sbuf("scaled", [P, J], F32)
-        xda = sbuf("xda", [P, J], F32)
+        from_a = sbuf("from_a", [P, J], F32)
         result = sbuf("result", [P, J], F32)
         for h in range(2):
             slots = slice(h * HALF, (h + 1) * HALF)
             entries = slice(h * HALF // 16, (h + 1) * HALF // 16)
-            nc.vector.tensor_tensor(scaled[:, slots], xdpa[:].indirect(list2[:, entries]), gain_wide[:, slots], ALU.mult)
+            nc.vector.tensor_tensor(from_a[:, slots], xdpa[:].indirect(list2[:, entries]), both_wide[:, slots], ALU.mult)
         for h in range(2):
             slots = slice(h * HALF, (h + 1) * HALF)
-            entries = slice(h * HALF // 16, (h + 1) * HALF // 16)
-            nc.vector.tensor_tensor(xda[:, slots], xdpb[:].indirect(list3[:, entries]), scaled[:, slots], ALU.add)
-        for h in range(2):
-            slots = slice(h * HALF, (h + 1) * HALF)
-            nc.vector.scalar_tensor_tensor(
-                result[:, slots], xda[:, slots], og_sb[:], base_sb[:, slots], ALU.mult, ALU.add
-            )
+            nc.vector.tensor_tensor(result[:, slots], from_a[:, slots], partial[:, slots], ALU.add)
             nc.sync.dma_start(out[:, slots], result[:, slots])

from contextlib import ExitStack

import concourse.mybir as mybir
from concourse.masks import make_identity

K, R, F, T, J, U = 512, 128, 512, 2048, 512, 1024
FLOPS = 2 * K * R * J * 2 + 2 * F * R * U

F32 = mybir.dt.float32
BF16 = mybir.dt.bfloat16
I32 = mybir.dt.int32
U32 = mybir.dt.uint32
U16 = mybir.dt.uint16
U8 = mybir.dt.uint8
FP8X4 = mybir.dt.float8_e4m3fn_x4
ALU = mybir.AluOpType
ACT = mybir.ActivationFunctionType

P = 128
PACK = 4
BANK = 512
HALF = J // 2
PER_BANK = BANK // P


def tile_attend_hvtwopages_kernel(
    tc, tab_words, tab_scales, w1, gain, ground, wo, dy, dtab_words, dtab_scales, og, base, offs, offs2, offs3, out
):
    nc = tc.nc
    with ExitStack() as ctx:
        sb = ctx.enter_context(tc.tile_pool(name="sb", bufs=1))
        ps = ctx.enter_context(tc.psum_pool(name="ps", bufs=1))

        def sbuf(name, shape, dtype, tag=""):
            return sb.tile(shape, dtype, name=name, align_bytes=64, tag=tag or name)

        def bank(name, number):
            return ps.tile([P, BANK], F32, name=name, tag="bank%d" % number)

        def load_words(name, words):
            t = sbuf(name, [P, T], U32)
            nc.sync.dma_start(t[:].bitcast(I32), words[0].rearrange("p n t -> p (n t)").bitcast(I32))
            return t

        def load_scales(t, scales):
            for q in range(4):
                nc.sync.dma_start(t[32 * q : 32 * q + 4, :].bitcast(I32), scales[0, 4 * q : 4 * q + 4, :].bitcast(I32))

        def load_plain(name, src, shape, dtype):
            t = sbuf(name, shape, dtype)
            nc.sync.dma_start(t[:], src)
            return t

        def load_rows(name, src):
            width = src.shape[1]
            t = sbuf(name, [P, PACK, width], F32)
            nc.sync.dma_start(t[:], src.rearrange("(p j) w -> p j w", j=PACK))
            return t

        def interleave(grouped, raw):
            nc.scalar.activation(
                grouped.rearrange("p (c i) j -> p c j i", i=4),
                raw.rearrange("p j (c i) -> p c j i", i=4),
                ACT.Copy,
            )

        def quantize(name, grouped):
            width = grouped.shape[1]
            codes = sbuf(name + "_codes", [P, width], U32)
            scales = sbuf(name + "_scales", [P, width], U8)
            nc.vector.quantize_mx(
                out=codes[:].bitcast(FP8X4), scales=scales[:], in_=grouped[:].rearrange("p w j -> p (w j)")
            )
            return codes, scales

        def product(acc, lhs, rhs_codes, rhs_scales):
            nc.tensor.matmul_mx(
                out=acc,
                lhsT=lhs[0][:].bitcast(FP8X4),
                lhsT_scale=lhs[1][:],
                rhs=rhs_codes.bitcast(FP8X4),
                rhs_scale=rhs_scales,
                start=True,
                stop=True,
            )

        def turn(dst, src, half, start, stop):
            for b in range(PER_BANK):
                lo = half * BANK + b * P
                nc.tensor.matmul(
                    dst[:, b * P : (b + 1) * P],
                    lhsT=src[:, lo : lo + P],
                    rhs=ident[:],
                    start=start and b == 0,
                    stop=stop and b == PER_BANK - 1,
                    is_transpose=True,
                )

        def halfcols(h):
            return slice(h * BANK, (h + 1) * BANK)

        ts_sb = sbuf("ts_sb", [P, T], U8)
        ds_sb = sbuf("ds_sb", [P, T], U8)
        nc.gpsimd.memset(ts_sb[:].bitcast(I32), 0)
        nc.vector.memset(ds_sb[:].bitcast(I32), 0)
        pb = sbuf("pb", [P, U], F32)
        pa = sbuf("pa", [P, U], F32)
        xpb = sbuf("xpb", [P, U], F32)
        xpa = sbuf("xpa", [P, U], F32)
        for page in (pb, pa, xpb, xpa):
            nc.vector.memset(page[:].bitcast(I32), 0)
        ident = sbuf("ident", [P, P], F32)
        make_identity(nc, ident[:])

        list1 = load_plain("list1", offs, [P, J // 16], U16)
        w1_raw = load_rows("w1_raw", w1)
        list3 = load_plain("list3", offs3, [P, J // 16], U16)
        load_scales(ts_sb, tab_scales)
        tw_sb = load_words("tw_sb", tab_words)
        load_scales(ds_sb, dtab_scales)
        dw_sb = load_words("dw_sb", dtab_words)
        list2 = load_plain("list2", offs2, [P, J // 16], U16)
        gain_sb = load_plain("gain_sb", gain, [P, 1], F32)
        wo_raw = load_rows("wo_raw", wo)
        dy_raw = [load_rows("dy_raw0", dy[:, halfcols(0)])]
        ground_sb = load_plain("ground_sb", ground, [P, U], F32)
        dy_raw.append(load_rows("dy_raw1", dy[:, halfcols(1)]))
        og_sb = load_plain("og_sb", og, [P, 1], F32)
        base_sb = load_plain("base_sb", base, [P, J], F32)

        w1_grouped = sbuf("w1_grouped", [P, R, PACK], BF16)
        interleave(w1_grouped[:], w1_raw[:])
        ts_g = sbuf("ts_g", [P, J], U8)
        nc.vector.tensor_copy(ts_g[:], ts_sb[:].indirect(list1[:]))
        w1_q = quantize("w1", w1_grouped)
        tw_g = sbuf("tw_g", [P, J], U32)
        a_sb = sbuf("a_sb", [P, J], F32)
        h1_sb = sbuf("h1_sb", [P, J], F32)
        a_ps = []
        for h in range(2):
            slots = slice(h * HALF, (h + 1) * HALF)
            entries = slice(h * HALF // 16, (h + 1) * HALF // 16)
            nc.vector.tensor_copy(tw_g[:, slots], tw_sb[:].indirect(list1[:, entries]))
            a_ps.append(bank("a_ps%d" % h, h))
            product(a_ps[h][:, :HALF], w1_q, tw_g[:, slots], ts_g[:, slots])
            nc.scalar.copy(a_sb[:, slots], a_ps[h][:, :HALF])
        for h in range(2):
            slots = slice(h * HALF, (h + 1) * HALF)
            nc.scalar.activation(h1_sb[:, slots], a_ps[h][:, :HALF], ACT.Copy, scale=gain_sb[:])
        ds_g = sbuf("ds_g", [P, J], U8)
        nc.vector.tensor_copy(ds_g[:], ds_sb[:].indirect(list1[:]))
        for h in range(2):
            slots = slice(h * HALF, (h + 1) * HALF)
            entries = slice(h * HALF // 16, (h + 1) * HALF // 16)
            nc.vector.tensor_copy(pb[:].indirect(list3[:, entries]), a_sb[:, slots])

        dw_g = sbuf("dw_g", [P, J], U32)
        nc.vector.tensor_copy(dw_g[:], dw_sb[:].indirect(list1[:]))
        ta_ps = bank("ta_ps", 6)
        product(ta_ps[:], w1_q, dw_g[:], ds_g[:])
        nc.vector.tensor_copy(pa[:].indirect(list2[:]), h1_sb[:])

        wo_grouped = sbuf("wo_grouped", [P, R, PACK], BF16)
        interleave(wo_grouped[:], wo_raw[:])
        wo_q = quantize("wo", wo_grouped)

        dy_grouped = [sbuf("dy_grouped%d" % h, [P, BANK, PACK], BF16) for h in range(2)]
        dy_q = []
        for h in range(2):
            for c in range(2):
                cols = slice(c * 256, (c + 1) * 256)
                interleave(dy_grouped[h][:, cols, :], dy_raw[h][:, :, cols])
            dy_q.append(quantize("dy%d" % h, dy_grouped[h]))
            if h == 0:
                ta_sb = sbuf("ta_sb", [P, J], F32, tag="dy_raw0")
                nc.scalar.copy(ta_sb[:], ta_ps[:])
                nc.vector.tensor_copy(xpb[:].indirect(list3[:]), ta_sb[:])
        late = sbuf("late", [P, J + U], F32, tag="dy_raw1")
        xh1_sb = late[:, :J]
        tanh_t = late[:, J:]
        nc.scalar.activation(xh1_sb, ta_ps[:], ACT.Copy, scale=gain_sb[:])
        nc.vector.tensor_copy(xpa[:].indirect(list2[:]), xh1_sb)

        q_ps = [bank("q_ps%d" % h, 2 + h) for h in range(2)]
        z_ps = [bank("z_ps%d" % h, 4 + h) for h in range(2)]
        for h in range(2):
            turn(z_ps[h], ground_sb, h, True, False)
        for h in range(2):
            turn(z_ps[h], pa, h, False, True)
            nc.scalar.activation(tanh_t[:, halfcols(h)], z_ps[h][:], ACT.Tanh)
        for h in range(2):
            turn(q_ps[h], ground_sb, h, True, False)
            turn(q_ps[h], pb, h, False, True)
        slope = sbuf("slope", [P, U], F32)
        tanh_sq = sbuf("tanh_sq", [P, U], F32)
        for h in range(2):
            back = bank("back%d" % h, h)
            turn(back, tanh_t, h, True, True)
            nc.scalar.activation(tanh_sq[:, halfcols(h)], back[:], ACT.Square)
        for h in range(2):
            nc.scalar.activation(slope[:, halfcols(h)], tanh_sq[:, halfcols(h)], ACT.Copy, scale=-1.0, bias=1.0)

        c0_ps = [bank("c0_ps%d" % h, h) for h in range(2)]
        for h in range(2):
            product(c0_ps[h][:], wo_q, dy_q[h][0][:], dy_q[h][1][:])

        xpb_t = sbuf("xpb_t", [P, U], F32)
        for h in range(2):
            turned = bank("xpb_ps%d" % h, 4 + h)
            turn(turned, xpb, h, True, True)
            nc.scalar.copy(xpb_t[:, halfcols(h)], turned[:])

        og_wide = sbuf("og_wide", [P, J], F32)
        nc.scalar.copy(og_wide[:], og_sb[:].to_broadcast([P, J]))
        both_wide = sbuf("both_wide", [P, J], F32)
        nc.scalar.activation(both_wide[:], og_wide[:], ACT.Copy, scale=gain_sb[:])

        xpa_ps = [bank("xpa_ps%d" % h, 4 + h) for h in range(2)]
        for h in range(2):
            turn(xpa_ps[h], xpa, h, True, True)
        sum_ps = [bank("sum_ps%d" % h, 6 + h) for h in range(2)]
        for h in range(2):
            turn(sum_ps[h], xpb_t, h, True, False)

        cs = sbuf("cs", [P, U], F32)
        w_t = sbuf("w_t", [P, U], F32)
        xdpb = sbuf("xdpb", [P, U], F32)
        xdpa = sbuf("xdpa", [P, U], F32)
        for h in range(2):
            nc.vector.tensor_tensor(cs[:, halfcols(h)], c0_ps[h][:], slope[:, halfcols(h)], ALU.mult)
            nc.gpsimd.tensor_tensor(xdpb[:, halfcols(h)], xpa[:, halfcols(h)], cs[:, halfcols(h)], ALU.mult)
        m_t = slope
        for h in range(2):
            nc.vector.scalar_tensor_tensor(
                m_t[:, halfcols(h)], q_ps[h][:], -2.0, tanh_t[:, halfcols(h)], ALU.mult, ALU.mult
            )
        for h in range(2):
            nc.vector.tensor_tensor(w_t[:, halfcols(h)], xpa_ps[h][:], m_t[:, halfcols(h)], ALU.mult)
            turn(sum_ps[h], w_t, h, False, True)
        from_b = slope[:, :J]
        partial = sbuf("partial", [P, J], F32)
        nc.vector.tensor_tensor(from_b, xdpb[:].indirect(list3[:]), og_wide[:], ALU.mult)
        for h in range(2):
            slots = slice(h * HALF, (h + 1) * HALF)
            nc.gpsimd.tensor_tensor(partial[:, slots], from_b[:, slots], base_sb[:, slots], ALU.add)
        for h in range(2):
            nc.vector.tensor_tensor(xdpa[:, halfcols(h)], sum_ps[h][:], cs[:, halfcols(h)], ALU.mult)

        from_a = sbuf("from_a", [P, J], F32)
        result = sbuf("result", [P, J], F32)
        for h in range(2):
            slots = slice(h * HALF, (h + 1) * HALF)
            entries = slice(h * HALF // 16, (h + 1) * HALF // 16)
            nc.vector.tensor_tensor(from_a[:, slots], xdpa[:].indirect(list2[:, entries]), both_wide[:, slots], ALU.mult)
        for h in range(2):
            slots = slice(h * HALF, (h + 1) * HALF)
            nc.vector.tensor_tensor(result[:, slots], from_a[:, slots], partial[:, slots], ALU.add)
            nc.sync.dma_start(out[:, slots], result[:, slots])
